import numpy as np
import ml_dtypes


def mxq(x, axis, fmt="e4m3"):
    dtype, down = {"e4m3": (ml_dtypes.float8_e4m3fn, 7), "e5m2": (ml_dtypes.float8_e5m2, 14)}[fmt]
    v = np.moveaxis(np.asarray(x, np.float32).astype(ml_dtypes.bfloat16).astype(np.float64), axis, -1)
    blocks = v.reshape(v.shape[:-1] + (-1, 32))
    amax = np.abs(blocks).max(-1, keepdims=True)
    byte = np.maximum(np.where(amax > 0, np.frexp(amax)[1] - 1 + 127, 0) - down, 1)
    scale = np.exp2(byte - 127.0)
    codes = (blocks / scale).astype(np.float32).astype(dtype).astype(np.float64)
    return np.moveaxis((codes * scale).reshape(v.shape), -1, axis)


WIDE = False


def mx_kscale(k):
    if not WIDE:
        return np.ones(k)
    levels = np.array([10, -10, 5, -5, 0])
    if k % 512:
        return np.exp2(np.random.permutation(np.resize(levels, k // 32))).repeat(32)
    a = np.empty((k // 512, 16))
    for p in range(k // 512):
        a[p, :8] = np.random.permutation(np.resize(levels, 8))
        for g in range(8):
            far = levels[np.abs(levels - a[p, g]) >= 10]
            a[p, g + 8] = far[np.random.randint(len(far))]
    return np.exp2(a.ravel()).repeat(32)


def f64(x):
    return np.asarray(x).astype(np.float64)


def striped(idx):
    return np.tile(idx.reshape(-1, 16).T, (8, 1)).astype(np.uint16)


def unstriped(offs):
    return offs[:16].T.reshape(-1).astype(np.int64)


E2M1 = np.array([0.0, 0.5, 1.0, 1.5, 2.0, 3.0, 4.0, 6.0, -0.0, -0.5, -1.0, -1.5, -2.0, -3.0, -4.0, -6.0])


def pack_weight(w, fmt):
    k, n = w.shape
    w = f64(np.asarray(w, np.float32).astype(ml_dtypes.bfloat16)).reshape(k // 32, 32, n)
    amax = np.abs(w).max(1)
    if fmt == "e4m3":
        byte = np.frexp(amax)[1] - 1 + 127 - 7
    else:
        mant, ex = np.frexp(amax / 6.0)
        byte = np.where(mant > 0.5, ex, ex - 1) + 127
    byte = np.clip(np.where(amax > 0, byte, 1), 1, 254)
    scaled = (w * np.exp2(127.0 - byte)[:, None, :]).reshape(k, n).astype(np.float32)
    by_word = np.ascontiguousarray(scaled.reshape(k // 512, 128, 4, n).transpose(0, 1, 3, 2))
    if fmt == "e4m3":
        words = by_word.astype(ml_dtypes.float8_e4m3fn).view(np.uint8)
    else:
        c = by_word.astype(ml_dtypes.float4_e2m1fn).view(np.uint8) & 0xF
        words = (c[..., 0::2] | (c[..., 1::2] << 4)).reshape(k // 512, 128, 2 * n)
    return np.ascontiguousarray(words), np.ascontiguousarray(byte.astype(np.uint8).reshape(k // 512, 16, n))


def unpack_weight(words, scales, fmt):
    g, _, n = scales.shape
    words = np.ascontiguousarray(words).reshape(g, 128, n, -1)
    if fmt == "e4m3":
        vals = words.view(ml_dtypes.float8_e4m3fn).astype(np.float64)
    else:
        nib = np.empty((g, 128, n, 4), np.uint8)
        nib[..., 0::2] = words & 0xF
        nib[..., 1::2] = words >> 4
        vals = E2M1[nib]
    vals = vals * np.repeat(np.exp2(scales.astype(np.float64) - 127.0), 8, axis=1)[..., None]
    return vals.transpose(0, 1, 3, 2).reshape(g * 512, n)


def gelu(v):
    return 0.5 * v * (1.0 + np.tanh(np.sqrt(2.0 / np.pi) * (v + 0.044715 * v**3)))


K, H, T, S, P = 1024, 512, 4096, 1024, 512


def setup_inputs():
    n = np.random.standard_normal
    s = mx_kscale(K)[:, None]
    u = mx_kscale(H)[:, None]
    tab_words, tab_scales = pack_weight(n((K, T)) * s, "e4m3")
    w4_words, w4_scales = pack_weight(n((K, H)) / np.sqrt(K) / s, "e2m1")
    m4_words, m4_scales = pack_weight(0.8 * n((H, P)) / np.sqrt(H) / u, "e2m1")
    return {
        "tab_words": tab_words, "tab_scales": tab_scales,
        "offs": striped(np.random.permutation(T)[:S]),
        "pos1": striped(np.random.permutation(S)[:P]),
        "pos2": striped(np.random.permutation(S)[:P]),
        "wa": (1.5 * n((K, H)) / np.sqrt(K) / s).astype(np.float32),
        "wb": (1.3 * n((K, H)) / np.sqrt(K) / s).astype(np.float32),
        "w4_words": w4_words, "w4_scales": w4_scales,
        "gain": (np.exp(0.3 * n(H)) * u[:, 0]).astype(np.float32),
        "vd": (0.8 * n(H) / np.sqrt(H) / u[:, 0] ** 2).astype(np.float32),
        "m4_words": m4_words, "m4_scales": m4_scales,
    }


def reference(tab_words, tab_scales, offs, pos1, pos2, wa, wb, w4_words, w4_scales, gain, vd, m4_words, m4_scales):
    v = unpack_weight(tab_words, tab_scales, "e4m3")[:, unstriped(offs)]
    w4 = unpack_weight(w4_words, w4_scales, "e2m1")
    m4 = unpack_weight(m4_words, m4_scales, "e2m1")
    form = mxq(f64(wa), 0, "e4m3").T @ v
    pace = mxq(f64(wb), 0, "e4m3").T @ v
    cap = w4.T @ v
    h = np.minimum(np.tanh(form) * pace, cap) * f64(gain)[:, None]
    x1 = mxq(h[:, unstriped(pos1)], 0, "e4m3")
    x2 = mxq(np.abs(h[:, unstriped(pos2)]) * f64(vd)[:, None], 0, "e4m3")
    e = x1.T @ x2 + x1.T @ m4
    return np.tanh(e)

@@ -1,0 +1,278 @@
+from contextlib import ExitStack
+
+import concourse.mybir as mybir
+
+K, H, T, S, NP = 1024, 512, 4096, 1024, 512
+FLOPS = 2 * (3 * K * H * S + 2 * H * NP * NP)
+
+F32 = mybir.dt.float32
+BF16 = mybir.dt.bfloat16
+I32 = mybir.dt.int32
+U32 = mybir.dt.uint32
+U16 = mybir.dt.uint16
+U8 = mybir.dt.uint8
+FP8X4 = mybir.dt.float8_e4m3fn_x4
+FP4X4 = mybir.dt.float4_e2m1fn_x4
+ACT = mybir.ActivationFunctionType
+ALU = mybir.AluOpType
+
+P = 128
+PACK = 4
+PASSES = K // (P * PACK)
+BANK = 512
+HALVES = S // BANK
+QUADS = 4
+
+
+def tile_list_line_match_advantage_kernel(
+    tc, tab_words, tab_scales, offs, pos1, pos2, wa, wb, w4_words, w4_scales, gain, vd, m4_words, m4_scales, out
+):
+    nc = tc.nc
+    with ExitStack() as ctx:
+        keep = ctx.enter_context(tc.tile_pool(name="keep", bufs=1))
+        work = ctx.enter_context(tc.tile_pool(name="work", bufs=4))
+        psum = ctx.enter_context(tc.psum_pool(name="psum", bufs=1))
+
+        def held(shape, dtype, name):
+            return keep.tile(shape, dtype, name=name, align_bytes=64)
+
+        offs_sb = keep.tile([P, S // 16], U16, name="offs_sb")
+        pos1_sb = keep.tile([P, NP // 16], U16, name="pos1_sb")
+        pos2_sb = keep.tile([P, NP // 16], U16, name="pos2_sb")
+        tab_w = [held([P, T], U32, f"tab_w{a}") for a in range(PASSES)]
+        tab_s = held([P, T], U8, "tab_s")
+        v_w = [held([P, S], U32, f"v_w{a}") for a in range(PASSES)]
+        v_s = held([P, S], U8, "v_s")
+        v_s1 = held([P, S], U8, "v_s1")
+        w4_raw = held([P, PASSES, 2 * H], U8, "w4_raw")
+        w4_raw_s = held([P, PASSES, H], U8, "w4_raw_s")
+        w4_w = held([P, PASSES, 2 * H], U8, "w4_w")
+        m4_w = held([P, 2 * NP], U8, "m4_w")
+        gain_sb = held([P, PACK], F32, "gain_sb")
+        vd_sb = held([P, PACK], F32, "vd_sb")
+
+        nc.vector.memset(tab_s[:].bitcast(I32), 0)
+        nc.vector.memset(w4_raw_s[:].rearrange("p a c -> p (a c)").bitcast(I32), 0)
+        nc.vector.memset(v_s1[:].bitcast(I32), 0)
+
+        def load_table(a, u):
+            cols = slice(u * T // 2, (u + 1) * T // 2)
+            words = tab_words[a].rearrange("p t i -> p (t i)").bitcast(I32)
+            nc.sync.dma_start(tab_w[a][:, cols].bitcast(I32), words[:, cols])
+
+        nc.sync.dma_start(offs_sb[:], offs)
+        nc.sync.dma_start(pos2_sb[:], pos2)
+        nc.sync.dma_start(pos1_sb[:], pos1)
+        nc.scalar.dma_start(w4_raw[:].bitcast(I32), w4_words.rearrange("a p c -> p a c").bitcast(I32))
+        nc.scalar.dma_start(gain_sb[:], gain.rearrange("(p t) -> p t", t=PACK))
+        nc.scalar.dma_start(vd_sb[:], vd.rearrange("(p t) -> p t", t=PACK))
+        nc.scalar.dma_start(m4_w[:].bitcast(I32), m4_words[0].bitcast(I32))
+
+        def load_weight(dst, w, a, m0, m1):
+            rows = w[a * P * PACK : (a + 1) * P * PACK, :].rearrange("(p j) c -> p j c", j=PACK)
+            view = dst.rearrange("p (j c) -> p j c", j=PACK)
+            nc.sync.dma_start(view, rows[:, :, PACK * m0 : PACK * m1])
+            return view
+
+        wa_raw = [held([P, PACK * H], F32, f"wa_raw{a}") for a in range(PASSES)]
+        wa0 = load_weight(wa_raw[0][:], wa, 0, 0, P)
+        for r in range(4):
+            nc.sync.dma_start(
+                tab_s[r:P:16, :].bitcast(I32), tab_scales[:, r:16:4, :].rearrange("a q c -> q a c").bitcast(I32)
+            )
+        load_table(0, 0)
+        load_table(0, 1)
+        wa1 = load_weight(wa_raw[1][:], wa, 1, 0, P)
+        load_table(1, 0)
+        load_table(1, 1)
+
+        for q in range(QUADS):
+            nc.gpsimd.dma_start(
+                w4_raw_s[32 * q : 32 * q + 4, :, :].bitcast(I32),
+                w4_scales[:, 4 * q : 4 * q + 4, :].rearrange("a r c -> r a c").bitcast(I32),
+            )
+
+        for a in range(PASSES):
+            nc.vector.tensor_copy(
+                w4_w[:, a, :].rearrange("p (t m b) -> p t m b", t=PACK, b=2),
+                w4_raw[:, a, :].rearrange("p (m t b) -> p t m b", t=PACK, b=2),
+            )
+
+        w_w = [held([P, PASSES, H], U32, f"w_w{wi}") for wi in range(2)]
+        w_s = [held([P, PASSES, H], U8, f"w_s{wi}") for wi in range(2)]
+
+        def prepare(wi, a, shares, cuts):
+            grouped = held([P, PACK, P, PACK], BF16, f"grouped{wi}{a}")
+            for copy, src, m0, m1 in shares:
+                copy(grouped[:, :, m0:m1, :].rearrange("p t m j -> p m t j"), src.rearrange("p j (m t) -> p m t j", t=PACK))
+            flat = grouped[:].rearrange("p t m j -> p (t m j)")
+            for c0, c1 in zip(cuts, cuts[1:]):
+                nc.vector.quantize_mx(
+                    w_w[wi][:, a, c0:c1].bitcast(FP8X4), w_s[wi][:, a, c0:c1], flat[:, PACK * c0 : PACK * c1]
+                )
+
+        def shared(src, cut):
+            return [(nc.scalar.copy, src[:, :, : PACK * cut], 0, cut), (nc.vector.tensor_copy, src[:, :, PACK * cut :], cut, P)]
+
+        def v_plane(a, cols):
+            return (v_s, v_s1)[a][:, cols]
+
+        def product(bank, wi, t, n):
+            cols = slice(n * BANK, (n + 1) * BANK)
+            rows = slice(t * P, (t + 1) * P)
+            for a in range(PASSES):
+                nc.tensor.matmul_mx(
+                    bank[:], lhsT=w_w[wi][:, a, rows].bitcast(FP8X4), lhsT_scale=w_s[wi][:, a, rows],
+                    rhs=v_w[a][:, cols].bitcast(FP8X4), rhs_scale=v_plane(a, cols),
+                    start=(a == 0), stop=(a == PASSES - 1),
+                )
+
+        def cap_product(bank, t, n):
+            cols = slice(n * BANK, (n + 1) * BANK)
+            for a in range(PASSES):
+                nc.tensor.matmul_mx(
+                    bank[:], lhsT=w4_w[:, a, 2 * t * P : 2 * (t + 1) * P].bitcast(FP4X4),
+                    lhsT_scale=w4_s[:, a, t * P : (t + 1) * P],
+                    rhs=v_w[a][:, cols].bitcast(FP8X4), rhs_scale=v_plane(a, cols),
+                    start=(a == 0), stop=(a == PASSES - 1),
+                )
+
+        prepare(0, 0, shared(wa0, 64), (0, H))
+        nc.vector.tensor_copy(v_s[:], tab_s[:].indirect(offs_sb[:]))
+        for r in range(4):
+            nc.sync.dma_start(v_s1[r:P:32, :].bitcast(I32), v_s[16 + r : P : 32, :].bitcast(I32))
+        nc.vector.tensor_copy(v_w[0][:], tab_w[0][:].indirect(offs_sb[:]))
+        wb_raw = held([P, PASSES * PACK * H], F32, "tab_w0")
+        size = PACK * H
+        wb0 = load_weight(wb_raw[:, 0:size], wb, 0, 0, P)
+        wb1_lo = load_weight(wb_raw[:, size : size + size // 2], wb, 1, 0, P // 2)
+        wb1_hi = load_weight(wb_raw[:, size + size // 2 : 2 * size], wb, 1, P // 2, P)
+        prepare(0, 1, shared(wa1, 64), (0, H))
+        w4_s = held([P, PASSES, H], U8, "w4_s")
+        nc.gpsimd.tensor_copy(
+            w4_s[:].rearrange("p a (t m) -> p a t m", t=PACK), w4_raw_s[:].rearrange("p a (m t) -> p a t m", t=PACK)
+        )
+        for n in range(HALVES):
+            nc.vector.tensor_copy(
+                v_w[1][:, n * BANK : (n + 1) * BANK], tab_w[1][:].indirect(offs_sb[:, n * BANK // 16 : (n + 1) * BANK // 16])
+            )
+        m4_s = held([P, NP], U8, "tab_w1")
+        nc.gpsimd.memset(m4_s[:].bitcast(I32), 0)
+        for q in range(QUADS):
+            nc.sync.dma_start(m4_s[32 * q : 32 * q + 4, :].bitcast(I32), m4_scales[0, 4 * q : 4 * q + 4, :].bitcast(I32))
+        prepare(1, 0, [(nc.vector.tensor_copy, wb0, 0, P)], (0, H))
+        prepare(
+            1, 1, [(nc.vector.tensor_copy, wb1_lo, 0, P // 2), (nc.vector.tensor_copy, wb1_hi, P // 2, P)], (0, P, H)
+        )
+
+        tform = [held([P, S], F32, f"tform{t}") for t in range(PACK)]
+        h = [held([P, S], F32, f"h{t}") for t in range(PACK)]
+        g1 = held([P, PACK, NP], F32, "g1")
+        x1_b0 = held([P, P, PACK], BF16, "x1_b0")
+        x2_b = held([P, NP, PACK], BF16, "x2_b")
+        x1_w = held([P, NP], U32, "x1_w")
+        x1_s = held([P, NP], U8, "x1_s")
+        x2_w = held([P, NP], U32, "x2_w")
+        x2_s = held([P, NP], U8, "x2_s")
+
+        banks = [psum.tile([P, BANK], F32, name=f"bank{b}") for b in range(8)]
+
+        def form_rows(t):
+            for n in range(HALVES):
+                bank = banks[HALVES * t + n]
+                product(bank, 0, t, n)
+                nc.scalar.activation(tform[t][:, n * BANK : (n + 1) * BANK], bank[:], ACT.Tanh)
+
+        g2 = held([P, PACK, NP], F32, "g2")
+        spare = held([P, 2, BANK], F32, "spare")
+        lows = held([P, 4, BANK], F32, "lows")
+        tp_at = {
+            (0, 0): spare[:, 0, :], (0, 1): spare[:, 1, :],
+            (1, 0): spare[:, 0, :], (1, 1): g2[:, 0, :],
+            (2, 0): g2[:, 1, :], (2, 1): g1[:, 0, :],
+            (3, 0): g2[:, 2, :], (3, 1): g1[:, 1, :],
+        }
+
+        def h_rows(t):
+            pace, cap = [], []
+            for n in range(HALVES):
+                pace.append(banks[(4 * t + n) % 8])
+                cap.append(banks[(4 * t + HALVES + n) % 8])
+                cap_product(cap[n], t, n)
+                product(pace[n], 1, t, n)
+            for n in range(HALVES):
+                nc.vector.tensor_tensor(tp_at[t, n], pace[n][:], tform[t][:, n * BANK : (n + 1) * BANK], ALU.mult)
+            for n in range(HALVES):
+                low = g1[:, 2, :] if (t, n) == (PACK - 1, HALVES - 1) else lows[:, (HALVES * t + n) % 4, :]
+                nc.vector.tensor_tensor(low, cap[n][:], tp_at[t, n], ALU.min)
+                nc.scalar.activation(h[t][:, n * BANK : (n + 1) * BANK], low, ACT.Copy, scale=gain_sb[:, t : t + 1])
+
+        def pick2(t):
+            nc.vector.tensor_copy(g2[:, t, :], h[t][:].indirect(pos2_sb[:]))
+            mag = work.tile([P, NP], F32, name="mag")
+            nc.scalar.activation(mag[:], g2[:, t, :], ACT.Abs)
+            nc.scalar.activation(x2_b[:, :, t], mag[:], ACT.Copy, scale=vd_sb[:, t : t + 1])
+
+        def pick1(t):
+            nc.vector.tensor_copy(g1[:, t, :], h[t][:].indirect(pos1_sb[:]))
+
+        for t in range(PACK):
+            form_rows(t)
+        h_rows(0)
+        h_rows(1)
+        pick2(0)
+        h_rows(2)
+        pick2(1)
+        pick1(0)
+        h_rows(3)
+        pick2(2)
+        pick1(1)
+        pick2(3)
+        pick1(2)
+
+        def pick1_last(i):
+            nc.vector.tensor_copy(
+                g1[:, PACK - 1, i * P : (i + 1) * P], h[PACK - 1][:].indirect(pos1_sb[:, i * P // 16 : (i + 1) * P // 16])
+            )
+
+        def x1_b(i):
+            return x1_b0[:] if i == 0 else x2_b[:, i * P : (i + 1) * P, :]
+
+        def round1(i):
+            cols = slice(i * P, (i + 1) * P)
+            nc.vector.tensor_copy(x1_b(i), g1[:, :, cols].rearrange("p t m -> p m t"))
+
+        def quant1(i):
+            cols = slice(i * P, (i + 1) * P)
+            nc.vector.quantize_mx(
+                x1_w[:, cols].bitcast(FP8X4), x1_s[:, cols], x1_b(i).rearrange("p m t -> p (m t)")
+            )
+
+        def score(i):
+            cols = slice(i * P, (i + 1) * P)
+            bank = banks[i]
+            nc.tensor.matmul_mx(
+                bank[:], lhsT=x1_w[:, cols].bitcast(FP8X4), lhsT_scale=x1_s[:, cols],
+                rhs=m4_w[:].bitcast(FP4X4), rhs_scale=m4_s[:], start=True, stop=False,
+            )
+            nc.tensor.matmul_mx(
+                bank[:], lhsT=x1_w[:, cols].bitcast(FP8X4), lhsT_scale=x1_s[:, cols],
+                rhs=x2_w[:].bitcast(FP8X4), rhs_scale=x2_s[:], start=False, stop=True,
+            )
+            res = work.tile([P, NP], F32, name="res")
+            nc.scalar.activation(res[:], bank[:], ACT.Tanh)
+            nc.sync.dma_start(out[cols, :], res[:])
+
+        blocks = NP // P
+        pick1_last(0)
+        round1(0)
+        pick1_last(1)
+        quant1(0)
+        nc.vector.quantize_mx(x2_w[:].bitcast(FP8X4), x2_s[:], x2_b[:].rearrange("p m t -> p (m t)"))
+        score(0)
+        for i in range(1, blocks):
+            round1(i)
+            if i + 1 < blocks:
+                pick1_last(i + 1)
+            quant1(i)
+            score(i)

@@ -117,14 +117,14 @@ def tile_list_line_match_advantage_kernel(
         def v_plane(a, cols):
             return (v_s, v_s1)[a][:, cols]
 
-        def product(bank, wi, t, n):
+        def product(bank, wi, t, n, order):
             cols = slice(n * BANK, (n + 1) * BANK)
             rows = slice(t * P, (t + 1) * P)
-            for a in range(PASSES):
+            for a in order:
                 nc.tensor.matmul_mx(
                     bank[:], lhsT=w_w[wi][:, a, rows].bitcast(FP8X4), lhsT_scale=w_s[wi][:, a, rows],
                     rhs=v_w[a][:, cols].bitcast(FP8X4), rhs_scale=v_plane(a, cols),
-                    start=(a == 0), stop=(a == PASSES - 1),
+                    start=(a == order[0]), stop=(a == order[-1]),
                 )
 
         def cap_product(bank, t, n):
@@ -168,7 +168,7 @@ def tile_list_line_match_advantage_kernel(
         tform = [held([P, S], F32, f"tform{t}") for t in range(PACK)]
         h = [held([P, S], F32, f"h{t}") for t in range(PACK)]
         g1 = held([P, PACK, NP], F32, "g1")
-        x1_b0 = held([P, P, PACK], BF16, "x1_b0")
+        x1_b0 = held([P, 2 * P, PACK], BF16, "x1_b0")
         x2_b = held([P, NP, PACK], BF16, "x2_b")
         x1_w = held([P, NP], U32, "x1_w")
         x1_s = held([P, NP], U8, "x1_s")
@@ -180,7 +180,7 @@ def tile_list_line_match_advantage_kernel(
         def form_rows(t):
             for n in range(HALVES):
                 bank = banks[HALVES * t + n]
-                product(bank, 0, t, n)
+                product(bank, 0, t, n, (0, 1))
                 nc.scalar.activation(tform[t][:, n * BANK : (n + 1) * BANK], bank[:], ACT.Tanh)
 
         g2 = held([P, PACK, NP], F32, "g2")
@@ -190,16 +190,17 @@ def tile_list_line_match_advantage_kernel(
             (0, 0): spare[:, 0, :], (0, 1): spare[:, 1, :],
             (1, 0): spare[:, 0, :], (1, 1): g2[:, 0, :],
             (2, 0): g2[:, 1, :], (2, 1): g1[:, 0, :],
-            (3, 0): g2[:, 2, :], (3, 1): g1[:, 1, :],
+            (3, 0): lows[:, 1, :], (3, 1): g1[:, 1, :],
         }
 
         def h_rows(t):
             pace, cap = [], []
             for n in range(HALVES):
-                pace.append(banks[(4 * t + n) % 8])
-                cap.append(banks[(4 * t + HALVES + n) % 8])
+                pace.append(banks[(4 * t + n) % 6])
+                product(pace[n], 1, t, n, (0, 1) if t == 0 else (1, 0))
+            for n in range(HALVES):
+                cap.append(banks[(4 * t + HALVES + n) % 6])
                 cap_product(cap[n], t, n)
-                product(pace[n], 1, t, n)
             for n in range(HALVES):
                 nc.vector.tensor_tensor(tp_at[t, n], pace[n][:], tform[t][:, n * BANK : (n + 1) * BANK], ALU.mult)
             for n in range(HALVES):
@@ -224,23 +225,24 @@ def tile_list_line_match_advantage_kernel(
         h_rows(2)
         pick2(1)
         pick1(0)
-        h_rows(3)
         pick2(2)
+        h_rows(3)
         pick1(1)
         pick2(3)
-        pick1(2)
 
-        def pick1_last(i):
+        def pick1_block(t, i):
             nc.vector.tensor_copy(
-                g1[:, PACK - 1, i * P : (i + 1) * P], h[PACK - 1][:].indirect(pos1_sb[:, i * P // 16 : (i + 1) * P // 16])
+                g1[:, t, i * P : (i + 1) * P], h[t][:].indirect(pos1_sb[:, i * P // 16 : (i + 1) * P // 16])
             )
 
         def x1_b(i):
-            return x1_b0[:] if i == 0 else x2_b[:, i * P : (i + 1) * P, :]
+            return (x1_b0 if i < 2 else x2_b)[:, i * P : (i + 1) * P, :]
 
         def round1(i):
             cols = slice(i * P, (i + 1) * P)
-            nc.vector.tensor_copy(x1_b(i), g1[:, :, cols].rearrange("p t m -> p m t"))
+            nc.vector.tensor_copy(
+                x1_b(i).rearrange("p (c e) t -> p c t e", e=4), g1[:, :, cols].rearrange("p t (c e) -> p c t e", e=4)
+            )
 
         def quant1(i):
             cols = slice(i * P, (i + 1) * P)
@@ -250,7 +252,7 @@ def tile_list_line_match_advantage_kernel(
 
         def score(i):
             cols = slice(i * P, (i + 1) * P)
-            bank = banks[i]
+            bank = banks[(6 + i) % 8]
             nc.tensor.matmul_mx(
                 bank[:], lhsT=x1_w[:, cols].bitcast(FP8X4), lhsT_scale=x1_s[:, cols],
                 rhs=m4_w[:].bitcast(FP4X4), rhs_scale=m4_s[:], start=True, stop=False,
@@ -264,15 +266,16 @@ def tile_list_line_match_advantage_kernel(
             nc.sync.dma_start(out[cols, :], res[:])
 
         blocks = NP // P
-        pick1_last(0)
-        round1(0)
-        pick1_last(1)
-        quant1(0)
-        nc.vector.quantize_mx(x2_w[:].bitcast(FP8X4), x2_s[:], x2_b[:].rearrange("p m t -> p (m t)"))
-        score(0)
-        for i in range(1, blocks):
+        pick1_block(2, 0)
+        pick1_block(3, 0)
+        for i in range(blocks):
             round1(i)
             if i + 1 < blocks:
-                pick1_last(i + 1)
+                pick1_block(2, i + 1)
+                pick1_block(3, i + 1)
             quant1(i)
-            score(i)
+            if i == 1:
+                nc.vector.quantize_mx(x2_w[:].bitcast(FP8X4), x2_s[:], x2_b[:].rearrange("p m t -> p (m t)"))
+                score(0)
+            if i >= 1:
+                score(i)

@@ -186,49 +186,67 @@ def tile_list_line_match_advantage_kernel(
         g2 = held([P, PACK, NP], F32, "g2")
         spare = held([P, 2, BANK], F32, "spare")
         lows = held([P, 4, BANK], F32, "lows")
+        late = held([P, 4, BANK], F32, "late")
+        pace_sb = held([P, 4, BANK], F32, "pace_sb")
         tp_at = {
             (0, 0): spare[:, 0, :], (0, 1): spare[:, 1, :],
             (1, 0): spare[:, 0, :], (1, 1): g2[:, 0, :],
-            (2, 0): g2[:, 1, :], (2, 1): g1[:, 0, :],
-            (3, 0): lows[:, 1, :], (3, 1): g1[:, 1, :],
+            (2, 0): late[:, 0, :], (2, 1): late[:, 1, :],
+            (3, 0): late[:, 2, :], (3, 1): late[:, 3, :],
         }
 
+        def times_on_vector(t):
+            for n in range(HALVES):
+                product(banks[4 * t + n], 1, t, n, (0, 1) if t == 0 else (1, 0))
+            for n in range(HALVES):
+                nc.vector.tensor_tensor(tp_at[t, n], banks[4 * t + n][:], tform[t][:, n * BANK : (n + 1) * BANK], ALU.mult)
+
+        def times_on_gpsimd(t):
+            for n in range(HALVES):
+                product(banks[6 + n], 1, t, n, (1, 0))
+                staged = pace_sb[:, HALVES * (t - 2) + n, :]
+                nc.scalar.copy(staged, banks[6 + n][:])
+                nc.gpsimd.tensor_tensor(tp_at[t, n], staged, tform[t][:, n * BANK : (n + 1) * BANK], ALU.mult)
+
         def h_rows(t):
-            pace, cap = [], []
+            cap = [banks[(2, 0, 2, 4)[t] + n] for n in range(HALVES)]
             for n in range(HALVES):
-                pace.append(banks[(4 * t + n) % 6])
-                product(pace[n], 1, t, n, (0, 1) if t == 0 else (1, 0))
-            for n in range(HALVES):
-                cap.append(banks[(4 * t + HALVES + n) % 6])
                 cap_product(cap[n], t, n)
             for n in range(HALVES):
-                nc.vector.tensor_tensor(tp_at[t, n], pace[n][:], tform[t][:, n * BANK : (n + 1) * BANK], ALU.mult)
-            for n in range(HALVES):
-                low = g1[:, 2, :] if (t, n) == (PACK - 1, HALVES - 1) else lows[:, (HALVES * t + n) % 4, :]
+                low = g1[:, 2 - n, :] if t == PACK - 1 else lows[:, (HALVES * t + n) % 4, :]
                 nc.vector.tensor_tensor(low, cap[n][:], tp_at[t, n], ALU.min)
                 nc.scalar.activation(h[t][:, n * BANK : (n + 1) * BANK], low, ACT.Copy, scale=gain_sb[:, t : t + 1])
+
+        x2_f = held([P, PACK, NP], F32, "x2_f")
+
+        def weave(copy, dst, src):
+            copy(dst.rearrange("p (c e) t -> p c t e", e=4), src.rearrange("p t (c e) -> p c t e", e=4))
 
         def pick2(t):
             nc.vector.tensor_copy(g2[:, t, :], h[t][:].indirect(pos2_sb[:]))
             mag = work.tile([P, NP], F32, name="mag")
             nc.scalar.activation(mag[:], g2[:, t, :], ACT.Abs)
-            nc.scalar.activation(x2_b[:, :, t], mag[:], ACT.Copy, scale=vd_sb[:, t : t + 1])
+            nc.scalar.activation(x2_f[:, t, :], mag[:], ACT.Copy, scale=vd_sb[:, t : t + 1])
 
         def pick1(t):
             nc.vector.tensor_copy(g1[:, t, :], h[t][:].indirect(pos1_sb[:]))
 
         for t in range(PACK):
             form_rows(t)
+        times_on_vector(0)
+        times_on_gpsimd(2)
         h_rows(0)
+        times_on_gpsimd(3)
+        times_on_vector(1)
         h_rows(1)
         pick2(0)
         h_rows(2)
         pick2(1)
         pick1(0)
-        pick2(2)
         h_rows(3)
-        pick1(1)
+        pick2(2)
         pick2(3)
+        pick1(1)
 
         def pick1_block(t, i):
             nc.vector.tensor_copy(
@@ -240,9 +258,7 @@ def tile_list_line_match_advantage_kernel(
 
         def round1(i):
             cols = slice(i * P, (i + 1) * P)
-            nc.vector.tensor_copy(
-                x1_b(i).rearrange("p (c e) t -> p c t e", e=4), g1[:, :, cols].rearrange("p t (c e) -> p c t e", e=4)
-            )
+            weave(nc.vector.tensor_copy, x1_b(i), g1[:, :, cols])
 
         def quant1(i):
             cols = slice(i * P, (i + 1) * P)
@@ -266,6 +282,7 @@ def tile_list_line_match_advantage_kernel(
             nc.sync.dma_start(out[cols, :], res[:])
 
         blocks = NP // P
+        weave(nc.scalar.copy, x2_b[:, : NP // 2, :], x2_f[:, :, : NP // 2])
         pick1_block(2, 0)
         pick1_block(3, 0)
         for i in range(blocks):
@@ -273,6 +290,8 @@ def tile_list_line_match_advantage_kernel(
             if i + 1 < blocks:
                 pick1_block(2, i + 1)
                 pick1_block(3, i + 1)
+            if i == 1:
+                weave(nc.vector.tensor_copy, x2_b[:, NP // 2 :, :], x2_f[:, :, NP // 2 :])
             quant1(i)
             if i == 1:
                 nc.vector.quantize_mx(x2_w[:].bitcast(FP8X4), x2_s[:], x2_b[:].rearrange("p m t -> p (m t)"))

from contextlib import ExitStack

import concourse.mybir as mybir

K, H, T, S, NP = 1024, 512, 4096, 1024, 512
FLOPS = 2 * (3 * K * H * S + 2 * H * NP * NP)

F32 = mybir.dt.float32
BF16 = mybir.dt.bfloat16
I32 = mybir.dt.int32
U32 = mybir.dt.uint32
U16 = mybir.dt.uint16
U8 = mybir.dt.uint8
FP8X4 = mybir.dt.float8_e4m3fn_x4
FP4X4 = mybir.dt.float4_e2m1fn_x4
ACT = mybir.ActivationFunctionType
ALU = mybir.AluOpType

P = 128
PACK = 4
PASSES = K // (P * PACK)
BANK = 512
HALVES = S // BANK
QUADS = 4


def tile_list_line_match_advantage_kernel(
    tc, tab_words, tab_scales, offs, pos1, pos2, wa, wb, w4_words, w4_scales, gain, vd, m4_words, m4_scales, out
):
    nc = tc.nc
    with ExitStack() as ctx:
        keep = ctx.enter_context(tc.tile_pool(name="keep", bufs=1))
        work = ctx.enter_context(tc.tile_pool(name="work", bufs=4))
        psum = ctx.enter_context(tc.psum_pool(name="psum", bufs=1))

        def held(shape, dtype, name):
            return keep.tile(shape, dtype, name=name, align_bytes=64)

        offs_sb = keep.tile([P, S // 16], U16, name="offs_sb")
        pos1_sb = keep.tile([P, NP // 16], U16, name="pos1_sb")
        pos2_sb = keep.tile([P, NP // 16], U16, name="pos2_sb")
        tab_w = [held([P, T], U32, f"tab_w{a}") for a in range(PASSES)]
        tab_s = held([P, T], U8, "tab_s")
        v_w = [held([P, S], U32, f"v_w{a}") for a in range(PASSES)]
        v_s = held([P, S], U8, "v_s")
        v_s1 = held([P, S], U8, "v_s1")
        w4_raw = held([P, PASSES, 2 * H], U8, "w4_raw")
        w4_raw_s = held([P, PASSES, H], U8, "w4_raw_s")
        w4_w = held([P, PASSES, 2 * H], U8, "w4_w")
        m4_w = held([P, 2 * NP], U8, "m4_w")
        gain_sb = held([P, PACK], F32, "gain_sb")
        vd_sb = held([P, PACK], F32, "vd_sb")

        nc.vector.memset(tab_s[:].bitcast(I32), 0)
        nc.vector.memset(w4_raw_s[:].rearrange("p a c -> p (a c)").bitcast(I32), 0)
        nc.vector.memset(v_s1[:].bitcast(I32), 0)

        def load_table(a, u):
            cols = slice(u * T // 2, (u + 1) * T // 2)
            words = tab_words[a].rearrange("p t i -> p (t i)").bitcast(I32)
            nc.sync.dma_start(tab_w[a][:, cols].bitcast(I32), words[:, cols])

        nc.sync.dma_start(offs_sb[:], offs)
        nc.sync.dma_start(pos2_sb[:], pos2)
        nc.sync.dma_start(pos1_sb[:], pos1)
        nc.scalar.dma_start(w4_raw[:].bitcast(I32), w4_words.rearrange("a p c -> p a c").bitcast(I32))
        nc.scalar.dma_start(gain_sb[:], gain.rearrange("(p t) -> p t", t=PACK))
        nc.scalar.dma_start(vd_sb[:], vd.rearrange("(p t) -> p t", t=PACK))
        nc.scalar.dma_start(m4_w[:].bitcast(I32), m4_words[0].bitcast(I32))

        def load_weight(dst, w, a, m0, m1):
            rows = w[a * P * PACK : (a + 1) * P * PACK, :].rearrange("(p j) c -> p j c", j=PACK)
            view = dst.rearrange("p (j c) -> p j c", j=PACK)
            nc.sync.dma_start(view, rows[:, :, PACK * m0 : PACK * m1])
            return view

        wa_raw = [held([P, PACK * H], F32, f"wa_raw{a}") for a in range(PASSES)]
        wa0 = load_weight(wa_raw[0][:], wa, 0, 0, P)
        for r in range(4):
            nc.sync.dma_start(
                tab_s[r:P:16, :].bitcast(I32), tab_scales[:, r:16:4, :].rearrange("a q c -> q a c").bitcast(I32)
            )
        load_table(0, 0)
        load_table(0, 1)
        wa1 = load_weight(wa_raw[1][:], wa, 1, 0, P)
        load_table(1, 0)
        load_table(1, 1)

        for q in range(QUADS):
            nc.gpsimd.dma_start(
                w4_raw_s[32 * q : 32 * q + 4, :, :].bitcast(I32),
                w4_scales[:, 4 * q : 4 * q + 4, :].rearrange("a r c -> r a c").bitcast(I32),
            )

        for a in range(PASSES):
            nc.vector.tensor_copy(
                w4_w[:, a, :].rearrange("p (t m b) -> p t m b", t=PACK, b=2),
                w4_raw[:, a, :].rearrange("p (m t b) -> p t m b", t=PACK, b=2),
            )

        w_w = [held([P, PASSES, H], U32, f"w_w{wi}") for wi in range(2)]
        w_s = [held([P, PASSES, H], U8, f"w_s{wi}") for wi in range(2)]

        def prepare(wi, a, shares, cuts):
            grouped = held([P, PACK, P, PACK], BF16, f"grouped{wi}{a}")
            for copy, src, m0, m1 in shares:
                copy(grouped[:, :, m0:m1, :].rearrange("p t m j -> p m t j"), src.rearrange("p j (m t) -> p m t j", t=PACK))
            flat = grouped[:].rearrange("p t m j -> p (t m j)")
            for c0, c1 in zip(cuts, cuts[1:]):
                nc.vector.quantize_mx(
                    w_w[wi][:, a, c0:c1].bitcast(FP8X4), w_s[wi][:, a, c0:c1], flat[:, PACK * c0 : PACK * c1]
                )

        def shared(src, cut):
            return [(nc.scalar.copy, src[:, :, : PACK * cut], 0, cut), (nc.vector.tensor_copy, src[:, :, PACK * cut :], cut, P)]

        def v_plane(a, cols):
            return (v_s, v_s1)[a][:, cols]

        def product(bank, wi, t, n, order):
            cols = slice(n * BANK, (n + 1) * BANK)
            rows = slice(t * P, (t + 1) * P)
            for a in order:
                nc.tensor.matmul_mx(
                    bank[:], lhsT=w_w[wi][:, a, rows].bitcast(FP8X4), lhsT_scale=w_s[wi][:, a, rows],
                    rhs=v_w[a][:, cols].bitcast(FP8X4), rhs_scale=v_plane(a, cols),
                    start=(a == order[0]), stop=(a == order[-1]),
                )

        def cap_product(bank, t, n):
            cols = slice(n * BANK, (n + 1) * BANK)
            for a in range(PASSES):
                nc.tensor.matmul_mx(
                    bank[:], lhsT=w4_w[:, a, 2 * t * P : 2 * (t + 1) * P].bitcast(FP4X4),
                    lhsT_scale=w4_s[:, a, t * P : (t + 1) * P],
                    rhs=v_w[a][:, cols].bitcast(FP8X4), rhs_scale=v_plane(a, cols),
                    start=(a == 0), stop=(a == PASSES - 1),
                )

        prepare(0, 0, shared(wa0, 64), (0, H))
        nc.vector.tensor_copy(v_s[:], tab_s[:].indirect(offs_sb[:]))
        for r in range(4):
            nc.sync.dma_start(v_s1[r:P:32, :].bitcast(I32), v_s[16 + r : P : 32, :].bitcast(I32))
        nc.vector.tensor_copy(v_w[0][:], tab_w[0][:].indirect(offs_sb[:]))
        wb_raw = held([P, PASSES * PACK * H], F32, "tab_w0")
        size = PACK * H
        wb0 = load_weight(wb_raw[:, 0:size], wb, 0, 0, P)
        wb1_lo = load_weight(wb_raw[:, size : size + size // 2], wb, 1, 0, P // 2)
        wb1_hi = load_weight(wb_raw[:, size + size // 2 : 2 * size], wb, 1, P // 2, P)
        prepare(0, 1, shared(wa1, 64), (0, H))
        w4_s = held([P, PASSES, H], U8, "w4_s")
        nc.gpsimd.tensor_copy(
            w4_s[:].rearrange("p a (t m) -> p a t m", t=PACK), w4_raw_s[:].rearrange("p a (m t) -> p a t m", t=PACK)
        )
        for n in range(HALVES):
            nc.vector.tensor_copy(
                v_w[1][:, n * BANK : (n + 1) * BANK], tab_w[1][:].indirect(offs_sb[:, n * BANK // 16 : (n + 1) * BANK // 16])
            )
        m4_s = held([P, NP], U8, "tab_w1")
        nc.gpsimd.memset(m4_s[:].bitcast(I32), 0)
        for q in range(QUADS):
            nc.sync.dma_start(m4_s[32 * q : 32 * q + 4, :].bitcast(I32), m4_scales[0, 4 * q : 4 * q + 4, :].bitcast(I32))
        prepare(1, 0, [(nc.vector.tensor_copy, wb0, 0, P)], (0, H))
        prepare(
            1, 1, [(nc.vector.tensor_copy, wb1_lo, 0, P // 2), (nc.vector.tensor_copy, wb1_hi, P // 2, P)], (0, P, H)
        )

        tform = [held([P, S], F32, f"tform{t}") for t in range(PACK)]
        h = [held([P, S], F32, f"h{t}") for t in range(PACK)]
        g1 = held([P, PACK, NP], F32, "g1")
        x1_b0 = held([P, 2 * P, PACK], BF16, "x1_b0")
        x2_b = held([P, NP, PACK], BF16, "x2_b")
        x1_w = held([P, NP], U32, "x1_w")
        x1_s = held([P, NP], U8, "x1_s")
        x2_w = held([P, NP], U32, "x2_w")
        x2_s = held([P, NP], U8, "x2_s")

        banks = [psum.tile([P, BANK], F32, name=f"bank{b}") for b in range(8)]

        def form_rows(t):
            for n in range(HALVES):
                bank = banks[HALVES * t + n]
                product(bank, 0, t, n, (0, 1))
                nc.scalar.activation(tform[t][:, n * BANK : (n + 1) * BANK], bank[:], ACT.Tanh)

        g2 = held([P, PACK, NP], F32, "g2")
        spare = held([P, 2, BANK], F32, "spare")
        lows = held([P, 4, BANK], F32, "lows")
        late = held([P, 4, BANK], F32, "late")
        pace_sb = held([P, 4, BANK], F32, "pace_sb")
        tp_at = {
            (0, 0): spare[:, 0, :], (0, 1): spare[:, 1, :],
            (1, 0): spare[:, 0, :], (1, 1): g2[:, 0, :],
            (2, 0): late[:, 0, :], (2, 1): late[:, 1, :],
            (3, 0): late[:, 2, :], (3, 1): late[:, 3, :],
        }

        def times_on_vector(t):
            for n in range(HALVES):
                product(banks[4 * t + n], 1, t, n, (0, 1) if t == 0 else (1, 0))
            for n in range(HALVES):
                nc.vector.tensor_tensor(tp_at[t, n], banks[4 * t + n][:], tform[t][:, n * BANK : (n + 1) * BANK], ALU.mult)

        def times_on_gpsimd(t):
            for n in range(HALVES):
                product(banks[6 + n], 1, t, n, (1, 0))
                staged = pace_sb[:, HALVES * (t - 2) + n, :]
                nc.scalar.copy(staged, banks[6 + n][:])
                nc.gpsimd.tensor_tensor(tp_at[t, n], staged, tform[t][:, n * BANK : (n + 1) * BANK], ALU.mult)

        def h_rows(t):
            cap = [banks[(2, 0, 2, 4)[t] + n] for n in range(HALVES)]
            for n in range(HALVES):
                cap_product(cap[n], t, n)
            for n in range(HALVES):
                low = g1[:, 2 - n, :] if t == PACK - 1 else lows[:, (HALVES * t + n) % 4, :]
                nc.vector.tensor_tensor(low, cap[n][:], tp_at[t, n], ALU.min)
                nc.scalar.activation(h[t][:, n * BANK : (n + 1) * BANK], low, ACT.Copy, scale=gain_sb[:, t : t + 1])

        x2_f = held([P, PACK, NP], F32, "x2_f")

        def weave(copy, dst, src):
            copy(dst.rearrange("p (c e) t -> p c t e", e=4), src.rearrange("p t (c e) -> p c t e", e=4))

        def pick2(t):
            nc.vector.tensor_copy(g2[:, t, :], h[t][:].indirect(pos2_sb[:]))
            mag = work.tile([P, NP], F32, name="mag")
            nc.scalar.activation(mag[:], g2[:, t, :], ACT.Abs)
            nc.scalar.activation(x2_f[:, t, :], mag[:], ACT.Copy, scale=vd_sb[:, t : t + 1])

        def pick1(t):
            nc.vector.tensor_copy(g1[:, t, :], h[t][:].indirect(pos1_sb[:]))

        for t in range(PACK):
            form_rows(t)
        times_on_vector(0)
        times_on_gpsimd(2)
        h_rows(0)
        times_on_gpsimd(3)
        times_on_vector(1)
        h_rows(1)
        pick2(0)
        h_rows(2)
        pick2(1)
        pick1(0)
        h_rows(3)
        pick2(2)
        pick2(3)
        pick1(1)

        def pick1_block(t, i):
            nc.vector.tensor_copy(
                g1[:, t, i * P : (i + 1) * P], h[t][:].indirect(pos1_sb[:, i * P // 16 : (i + 1) * P // 16])
            )

        def x1_b(i):
            return (x1_b0 if i < 2 else x2_b)[:, i * P : (i + 1) * P, :]

        def round1(i):
            cols = slice(i * P, (i + 1) * P)
            weave(nc.vector.tensor_copy, x1_b(i), g1[:, :, cols])

        def quant1(i):
            cols = slice(i * P, (i + 1) * P)
            nc.vector.quantize_mx(
                x1_w[:, cols].bitcast(FP8X4), x1_s[:, cols], x1_b(i).rearrange("p m t -> p (m t)")
            )

        def score(i):
            cols = slice(i * P, (i + 1) * P)
            bank = banks[(6 + i) % 8]
            nc.tensor.matmul_mx(
                bank[:], lhsT=x1_w[:, cols].bitcast(FP8X4), lhsT_scale=x1_s[:, cols],
                rhs=m4_w[:].bitcast(FP4X4), rhs_scale=m4_s[:], start=True, stop=False,
            )
            nc.tensor.matmul_mx(
                bank[:], lhsT=x1_w[:, cols].bitcast(FP8X4), lhsT_scale=x1_s[:, cols],
                rhs=x2_w[:].bitcast(FP8X4), rhs_scale=x2_s[:], start=False, stop=True,
            )
            res = work.tile([P, NP], F32, name="res")
            nc.scalar.activation(res[:], bank[:], ACT.Tanh)
            nc.sync.dma_start(out[cols, :], res[:])

        blocks = NP // P
        weave(nc.scalar.copy, x2_b[:, : NP // 2, :], x2_f[:, :, : NP // 2])
        pick1_block(2, 0)
        pick1_block(3, 0)
        for i in range(blocks):
            round1(i)
            if i + 1 < blocks:
                pick1_block(2, i + 1)
                pick1_block(3, i + 1)
            if i == 1:
                weave(nc.vector.tensor_copy, x2_b[:, NP // 2 :, :], x2_f[:, :, NP // 2 :])
            quant1(i)
            if i == 1:
                nc.vector.quantize_mx(x2_w[:].bitcast(FP8X4), x2_s[:], x2_b[:].rearrange("p m t -> p (m t)"))
                score(0)
            if i >= 1:
                score(i)
